import numpy as np
import ml_dtypes


def mxq(x, axis, fmt="e4m3"):
    dtype, down = {"e4m3": (ml_dtypes.float8_e4m3fn, 7), "e5m2": (ml_dtypes.float8_e5m2, 14)}[fmt]
    v = np.moveaxis(np.asarray(x, np.float32).astype(ml_dtypes.bfloat16).astype(np.float64), axis, -1)
    blocks = v.reshape(v.shape[:-1] + (-1, 32))
    amax = np.abs(blocks).max(-1, keepdims=True)
    byte = np.maximum(np.where(amax > 0, np.frexp(amax)[1] - 1 + 127, 0) - down, 1)
    scale = np.exp2(byte - 127.0)
    codes = (blocks / scale).astype(np.float32).astype(dtype).astype(np.float64)
    return np.moveaxis((codes * scale).reshape(v.shape), -1, axis)


WIDE = False


def mx_kscale(k):
    if not WIDE:
        return np.ones(k)
    levels = np.array([30, -30])
    if k % 512:
        return np.exp2(np.random.permutation(np.resize(levels, k // 32))).repeat(32)
    a = np.empty((k // 512, 16))
    for p in range(k // 512):
        a[p, :8] = np.random.permutation(np.resize(levels, 8))
        for g in range(8):
            far = levels[np.abs(levels - a[p, g]) >= 10]
            a[p, g + 8] = far[np.random.randint(len(far))]
    return np.exp2(a.ravel()).repeat(32)


def f64(x):
    return np.asarray(x).astype(np.float64)


def striped(idx):
    return np.tile(np.asarray(idx).reshape(-1, 16).T, (8, 1)).astype(np.uint16)


def unstriped(offs):
    return offs[:16].T.reshape(-1).astype(np.int64)


E2M1 = np.array([0.0, 0.5, 1.0, 1.5, 2.0, 3.0, 4.0, 6.0, -0.0, -0.5, -1.0, -1.5, -2.0, -3.0, -4.0, -6.0])


def pack_weight(w, fmt):
    k, n = w.shape
    w = f64(np.asarray(w, np.float32).astype(ml_dtypes.bfloat16)).reshape(k // 32, 32, n)
    amax = np.abs(w).max(1)
    if fmt in ("e4m3", "e5m2"):
        byte = np.frexp(amax)[1] - 1 + 127 - (7 if fmt == "e4m3" else 14)
    else:
        mant, ex = np.frexp(amax / 6.0)
        byte = np.where(mant > 0.5, ex, ex - 1) + 127
    byte = np.clip(np.where(amax > 0, byte, 1), 1, 254)
    scaled = (w * np.exp2(127.0 - byte)[:, None, :]).reshape(k, n).astype(np.float32)
    by_word = np.ascontiguousarray(scaled.reshape(k // 512, 128, 4, n).transpose(0, 1, 3, 2))
    if fmt in ("e4m3", "e5m2"):
        words = by_word.astype(ml_dtypes.float8_e4m3fn if fmt == "e4m3" else ml_dtypes.float8_e5m2).view(np.uint8)
    else:
        c = by_word.astype(ml_dtypes.float4_e2m1fn).view(np.uint8) & 0xF
        words = (c[..., 0::2] | (c[..., 1::2] << 4)).reshape(k // 512, 128, 2 * n)
    return np.ascontiguousarray(words), np.ascontiguousarray(byte.astype(np.uint8).reshape(k // 512, 16, n))


def unpack_weight(words, scales, fmt):
    g, _, n = scales.shape
    words = np.ascontiguousarray(words).reshape(g, 128, n, -1)
    if fmt in ("e4m3", "e5m2"):
        vals = words.view(ml_dtypes.float8_e4m3fn if fmt == "e4m3" else ml_dtypes.float8_e5m2).astype(np.float64)
    else:
        nib = np.empty((g, 128, n, 4), np.uint8)
        nib[..., 0::2] = words & 0xF
        nib[..., 1::2] = words >> 4
        vals = E2M1[nib]
    vals = vals * np.repeat(np.exp2(scales.astype(np.float64) - 127.0), 8, axis=1)[..., None]
    return vals.transpose(0, 1, 3, 2).reshape(g * 512, n)


def sigmoid(v):
    return 1.0 / (1.0 + np.exp(-v))


K, T, Z, J, R, Q, N, L = 512, 1024, 1024, 256, 512, 1024, 256, 512


def setup_inputs():
    n = np.random.standard_normal
    idx = np.random.permutation(T)[:J]
    idx2 = np.random.permutation(Z)[:J]
    idx3 = np.random.permutation(Q)[:J]
    fk = mx_kscale(K)
    fr = mx_kscale(R)
    fl = mx_kscale(L)
    xtp = pack_weight(n((K, T)) / fk[:, None], "e4m3")
    xop = pack_weight(n((K, Z)) / fk[:, None], "e2m1")
    wp = pack_weight(n((K, R)) * 1 / np.sqrt(K) * fk[:, None] * fr, "e5m2")
    w2p = pack_weight(n((K, R)) * 1 / np.sqrt(K) * fk[:, None] * fr, "e5m2")
    wbp = pack_weight(n((R, N)) * 1 / np.sqrt(R) / fr[:, None], "e5m2")
    sxp = pack_weight(n((L, J)) / fl[:, None], "e2m1")
    wsp = pack_weight(n((L, N)) * 1 / np.sqrt(L) * fl[:, None], "e5m2")
    return {
        "xt_words": xtp[0],
        "xt_scales": xtp[1],
        "xo_words": xop[0],
        "xo_scales": xop[1],
        "w_words": wp[0],
        "w_scales": wp[1],
        "w2_words": w2p[0],
        "w2_scales": w2p[1],
        "tg": (1.0 * n((R, Q))).astype(np.float32),
        "sg": (np.random.uniform(0.6, 1.6, (R, 1))).astype(np.float32),
        "bg": (np.random.uniform(-1.0, 1.0, (R, 1))).astype(np.float32),
        "wb_words": wbp[0],
        "wb_scales": wbp[1],
        "sx_words": sxp[0],
        "sx_scales": sxp[1],
        "ws_words": wsp[0],
        "ws_scales": wsp[1],
        "offs": striped(idx),
        "offs2": striped(idx2),
        "offs3": striped(idx3),
    }


def reference(xt_words, xt_scales, xo_words, xo_scales, w_words, w_scales, w2_words, w2_scales, tg, sg, bg, wb_words, wb_scales, sx_words, sx_scales, ws_words, ws_scales, offs, offs2, offs3):
    idx = unstriped(offs)
    idx2 = unstriped(offs2)
    idx3 = unstriped(offs3)
    xtu = unpack_weight(xt_words, xt_scales, "e4m3")
    xou = unpack_weight(xo_words, xo_scales, "e2m1")
    wu = unpack_weight(w_words, w_scales, "e5m2")
    w2u = unpack_weight(w2_words, w2_scales, "e5m2")
    wbu = unpack_weight(wb_words, wb_scales, "e5m2")
    sxu = unpack_weight(sx_words, sx_scales, "e2m1")
    wsu = unpack_weight(ws_words, ws_scales, "e5m2")
    xtidxg = xtu[:, idx]
    xoidx2g = xou[:, idx2]
    a = wu.T @ xtidxg + w2u.T @ xoidx2g
    b = w2u.T @ xtidxg + wu.T @ xoidx2g
    hid = np.maximum(a, b) * sigmoid(f64(tg)[:, idx3] * f64(sg) + f64(bg))
    hidq = mxq(hid, 0, "e4m3")
    y = wbu.T @ hidq + wsu.T @ sxu
    return y

@@ -1,0 +1,173 @@
+from contextlib import ExitStack
+
+import concourse.mybir as mybir
+from concourse.masks import make_identity
+
+K, T, J, R, N = 512, 1024, 256, 512, 256
+FLOPS = 2 * K * (4 * R * J + 2 * N * J)
+
+F32 = mybir.dt.float32
+BF16 = mybir.dt.bfloat16
+I32 = mybir.dt.int32
+U32 = mybir.dt.uint32
+U16 = mybir.dt.uint16
+U8 = mybir.dt.uint8
+E4M3 = mybir.dt.float8_e4m3fn_x4
+E5M2 = mybir.dt.float8_e5m2_x4
+E2M1 = mybir.dt.float4_e2m1fn_x4
+ALU = mybir.AluOpType
+ACT = mybir.ActivationFunctionType
+
+P = 128
+PACK = 4
+HALF = 128
+SCALE_ROWS = 16
+TOP = P - SCALE_ROWS
+
+
+def tile_list_crossed_tablegate_skip_plain_kernel(
+    tc, xt_words, xt_scales, xo_words, xo_scales, w_words, w_scales, w2_words, w2_scales, tg, sg, bg,
+    wb_words, wb_scales, sx_words, sx_scales, ws_words, ws_scales, offs, offs2, offs3, out,
+):
+    nc = tc.nc
+
+    def words8(dram):
+        return dram[0].rearrange("p n t -> p (n t)").bitcast(I32)
+
+    def spread_rows(queue, planes, first_row):
+        view = planes[:].bitcast(I32)
+        for q in range(4):
+            row = first_row + 4 * q
+            if row != 32 * q:
+                queue.dma_start(out=view[32 * q : 32 * q + 4, :], in_=view[row : row + 4, :])
+
+    with ExitStack() as ctx:
+        keep = ctx.enter_context(tc.tile_pool(name="keep", bufs=1))
+        reuse = ctx.enter_context(tc.tile_pool(name="reuse", bufs=1))
+        psum = ctx.enter_context(tc.psum_pool(name="psum", bufs=1))
+
+        list_t = keep.tile([P, J // 16], U16, name="list_t")
+        list_o = keep.tile([P, J // 16], U16, name="list_o")
+        list_g = keep.tile([P, J // 16], U16, name="list_g")
+        xt_win = reuse.tile([P, T], U32, name="xt_win", align_bytes=64, offset=0)
+        xo_win = reuse.tile([P, T], U16, name="xo_win", align_bytes=64, offset=7936)
+        xts_win = keep.tile([P, T], U8, name="xts_win", align_bytes=64)
+        xos_win = keep.tile([P, T], U8, name="xos_win", align_bytes=64)
+        xt_got = keep.tile([P, J], U32, name="xt_got", align_bytes=64)
+        xo_got = keep.tile([P, J], U16, name="xo_got", align_bytes=64)
+        xts_got = keep.tile([P, J], U8, name="xts_got", align_bytes=64)
+        xos_got = keep.tile([P, J], U8, name="xos_got", align_bytes=64)
+        w_sb = keep.tile([P, R], U32, name="w_sb", align_bytes=64)
+        w2_sb = keep.tile([P, R], U32, name="w2_sb", align_bytes=64)
+        wb_sb = reuse.tile([P, N], U32, name="wb_sb", align_bytes=64, offset=14336)
+        ws_sb = reuse.tile([P, N], U32, name="ws_sb", align_bytes=64, offset=8704)
+        sx_sb = reuse.tile([P, J], U16, name="sx_sb", align_bytes=64, offset=8192)
+        early = keep.tile([P, 2 * J + 2 * R], U8, name="early", align_bytes=64)
+        late = keep.tile([P, 2 * N + J], U8, name="late", align_bytes=64)
+        slope = keep.tile([P, PACK], F32, name="slope")
+        offset = keep.tile([P, PACK], F32, name="offset")
+        ident = keep.tile([P, P], F32, name="ident")
+        tg_win = [keep.tile([P, T], F32, name="tg_win0")]
+        tg_win.extend(reuse.tile([P, T], F32, name="tg_win%d" % t, align_bytes=64, offset=(0, 4096, 9728)[t - 1]) for t in range(1, PACK))
+        gate = keep.tile([P, PACK, J], F32, name="gate", align_bytes=64)
+
+        xt_cols, xo_cols = slice(0, J), slice(J, 2 * J)
+        w_cols, w2_cols = slice(2 * J, 2 * J + R), slice(2 * J + R, 2 * J + 2 * R)
+        wb_at, ws_at, sx_at = 0, N, 2 * N
+
+        nc.vector.memset(xts_win[0:TOP, :].bitcast(I32), 0)
+        nc.vector.memset(xos_win[0:TOP, :].bitcast(I32), 0)
+        nc.vector.memset(early[0:TOP, 2 * J :].bitcast(I32), 0)
+        nc.gpsimd.memset(late[:].bitcast(I32), 0)
+
+        nc.sync.dma_start(list_t[:], offs)
+        nc.scalar.dma_start(out=xts_win[TOP:P, :].bitcast(I32), in_=xt_scales[0].bitcast(I32))
+        nc.sync.dma_start(list_o[:], offs2)
+        nc.scalar.dma_start(out=xos_win[TOP:P, :].bitcast(I32), in_=xo_scales[0].bitcast(I32))
+        nc.sync.dma_start(out=xt_win[:].bitcast(I32), in_=words8(xt_words))
+        nc.scalar.dma_start(out=early[TOP:P, w_cols].bitcast(I32), in_=w_scales[0].bitcast(I32))
+        nc.scalar.dma_start(out=early[TOP:P, w2_cols].bitcast(I32), in_=w2_scales[0].bitcast(I32))
+        nc.sync.dma_start(out=xo_win[:].bitcast(I32), in_=xo_words[0].bitcast(I32))
+        nc.sync.dma_start(out=w_sb[:].bitcast(I32), in_=words8(w_words))
+        nc.sync.dma_start(out=w2_sb[:].bitcast(I32), in_=words8(w2_words))
+        nc.sync.dma_start(list_g[:], offs3)
+
+        nc.gpsimd.dma_start(out=slope[:], in_=sg.rearrange("(p t) o -> p (t o)", t=PACK))
+        nc.gpsimd.dma_start(out=offset[:], in_=bg.rearrange("(p t) o -> p (t o)", t=PACK))
+        for at, scales in ((wb_at, wb_scales), (ws_at, ws_scales), (sx_at, sx_scales)):
+            nc.gpsimd.dma_start(out=late[0:SCALE_ROWS, at : at + N].bitcast(I32), in_=scales[0].bitcast(I32))
+        make_identity(nc, ident[:])
+        spread_rows(nc.gpsimd, late, 0)
+
+        nc.vector.tensor_copy(xts_got[:], xts_win[:].indirect(list_t[:]))
+        nc.vector.tensor_copy(xos_got[:], xos_win[:].indirect(list_o[:]))
+        nc.vector.tensor_copy(early[:, xt_cols].bitcast(I32), xts_got[:].bitcast(I32))
+        nc.vector.tensor_copy(early[:, xo_cols].bitcast(I32), xos_got[:].bitcast(I32))
+        spread_rows(nc.scalar, early, TOP)
+        nc.vector.tensor_copy(xt_got[:], xt_win[:].indirect(list_t[:]))
+        nc.vector.tensor_copy(xo_got[:], xo_win[:].indirect(list_o[:]))
+
+        tg_rows = tg.rearrange("(p t) q -> p t q", t=PACK)
+        for t in range(PACK):
+            nc.sync.dma_start(out=tg_win[t][:], in_=tg_rows[:, t, :])
+        nc.sync.dma_start(out=ws_sb[:].bitcast(I32), in_=words8(ws_words))
+        nc.sync.dma_start(out=sx_sb[:].bitcast(I32), in_=sx_words[0].bitcast(I32))
+
+        for t in range(PACK):
+            nc.scalar.activation(
+                out=gate[:, t, :], in_=tg_win[t][:].indirect(list_g[:]), func=ACT.Sigmoid,
+                bias=offset[:, t : t + 1], scale=slope[:, t : t + 1],
+            )
+
+        turned = []
+        for h in range(J // HALF):
+            js = slice(h * HALF, (h + 1) * HALF)
+            xt_op = (xt_got[:, js].bitcast(E4M3), early[:, h * HALF : (h + 1) * HALF])
+            xo_op = (xo_got[:, js].bitcast(E2M1), early[:, J + h * HALF : J + (h + 1) * HALF])
+            w_op = (w_sb[:].bitcast(E5M2), early[:, w_cols])
+            w2_op = (w2_sb[:].bitcast(E5M2), early[:, w2_cols])
+            a_ps = psum.tile([P, R], F32, name="a_ps%d" % h)
+            b_ps = psum.tile([P, R], F32, name="b_ps%d" % h, tag="b_ps%d" % h)
+            for acc, with_xt, with_xo in ((a_ps, w_op, w2_op), (b_ps, w2_op, w_op)):
+                nc.tensor.matmul_mx(out=acc[:], lhsT=xt_op[0], lhsT_scale=xt_op[1], rhs=with_xt[0], rhs_scale=with_xt[1], start=True, stop=False)
+                nc.tensor.matmul_mx(out=acc[:], lhsT=xo_op[0], lhsT_scale=xo_op[1], rhs=with_xo[0], rhs_scale=with_xo[1], start=False, stop=True)
+            a_sb = reuse.tile([P, PACK, P], F32, name="a_sb%d" % h, align_bytes=64, offset=14336 + 2048 * h)
+            larger = keep.tile([P, PACK, P], F32, name="larger%d" % h)
+            nc.vector.tensor_copy(a_sb[:], a_ps[:].rearrange("j (m t) -> j t m", t=PACK))
+            nc.vector.tensor_tensor(larger[:], b_ps[:].rearrange("j (m t) -> j t m", t=PACK), a_sb[:], ALU.max)
+            turned.append(larger)
+        nc.sync.dma_start(out=wb_sb[:].bitcast(I32), in_=words8(wb_words))
+
+        out_rows = out.rearrange("(c p) j -> p c j", p=P)
+        backs = []
+        for h in range(J // HALF):
+            back = psum.tile([P, PACK, HALF], F32, name="back%d" % h, tag="back%d" % h)
+            for t in range(PACK):
+                nc.tensor.transpose(back[:, t, :], turned[h][:, t, :], ident[:])
+            backs.append(back)
+        for h in range(J // HALF):
+            js = slice(h * HALF, (h + 1) * HALF)
+            back = backs[h]
+            hid = keep.tile([P, HALF, PACK], BF16, name="hid%d" % h, align_bytes=64)
+            nc.vector.tensor_tensor(hid[:], back[:].rearrange("p t j -> p j t"), gate[:, :, js].rearrange("p t j -> p j t"), ALU.mult)
+            codes = keep.tile([P, HALF], U32, name="codes%d" % h, align_bytes=64)
+            plane = keep.tile([P, HALF], U8, name="plane%d" % h, align_bytes=64)
+            nc.vector.quantize_mx(out=codes[:].bitcast(E4M3), scales=plane[:], in_=hid[:].rearrange("p j t -> p (j t)"))
+            y_ps = psum.tile([P, N // P, HALF], F32, name="y_ps%d" % h, tag=("b_ps1", "back0")[h])
+            for c in range(N // P):
+                nc.tensor.matmul_mx(
+                    out=y_ps[:, c, :], lhsT=ws_sb[:, c * P : (c + 1) * P].bitcast(E5M2), lhsT_scale=late[:, ws_at + c * P : ws_at + (c + 1) * P],
+                    rhs=sx_sb[:, js].bitcast(E2M1), rhs_scale=late[:, sx_at + h * HALF : sx_at + (h + 1) * HALF], start=(c == 0), stop=False,
+                )
+            for c in range(N // P):
+                nc.tensor.matmul_mx(
+                    out=y_ps[:, c, :], lhsT=wb_sb[:, c * P : (c + 1) * P].bitcast(E5M2), lhsT_scale=late[:, wb_at + c * P : wb_at + (c + 1) * P],
+                    rhs=codes[:].bitcast(E4M3), rhs_scale=plane[:], start=False, stop=(c == N // P - 1),
+                )
+            y_sb = keep.tile([P, N // P, HALF], F32, name="y_sb%d" % h)
+            if h == 0:
+                nc.scalar.copy(y_sb[:], y_ps[:])
+                nc.scalar.dma_start(out=out_rows[:, :, js], in_=y_sb[:])
+            else:
+                nc.vector.tensor_copy(y_sb[:], y_ps[:])
+                nc.sync.dma_start(out=out_rows[:, :, js], in_=y_sb[:])

@@ -34,12 +34,10 @@ def tile_list_crossed_tablegate_skip_plain_kernel(
     def words8(dram):
         return dram[0].rearrange("p n t -> p (n t)").bitcast(I32)
 
-    def spread_rows(queue, planes, first_row):
-        view = planes[:].bitcast(I32)
+    def spread_rows(queue, planes, source, first_row):
         for q in range(4):
             row = first_row + 4 * q
-            if row != 32 * q:
-                queue.dma_start(out=view[32 * q : 32 * q + 4, :], in_=view[row : row + 4, :])
+            queue.dma_start(out=planes[32 * q : 32 * q + 4, :].bitcast(I32), in_=source[row : row + 4, :].bitcast(I32))
 
     with ExitStack() as ctx:
         keep = ctx.enter_context(tc.tile_pool(name="keep", bufs=1))
@@ -49,8 +47,8 @@ def tile_list_crossed_tablegate_skip_plain_kernel(
         list_t = keep.tile([P, J // 16], U16, name="list_t")
         list_o = keep.tile([P, J // 16], U16, name="list_o")
         list_g = keep.tile([P, J // 16], U16, name="list_g")
-        xt_win = reuse.tile([P, T], U32, name="xt_win", align_bytes=64, offset=0)
-        xo_win = reuse.tile([P, T], U16, name="xo_win", align_bytes=64, offset=7936)
+        xt_win = reuse.tile([P, T], U32, name="xt_win", align_bytes=64, offset=2048)
+        xo_win = reuse.tile([P, T], U16, name="xo_win", align_bytes=64, offset=12736)
         xts_win = keep.tile([P, T], U8, name="xts_win", align_bytes=64)
         xos_win = keep.tile([P, T], U8, name="xos_win", align_bytes=64)
         xt_got = keep.tile([P, J], U32, name="xt_got", align_bytes=64)
@@ -59,16 +57,17 @@ def tile_list_crossed_tablegate_skip_plain_kernel(
         xos_got = keep.tile([P, J], U8, name="xos_got", align_bytes=64)
         w_sb = keep.tile([P, R], U32, name="w_sb", align_bytes=64)
         w2_sb = keep.tile([P, R], U32, name="w2_sb", align_bytes=64)
-        wb_sb = reuse.tile([P, N], U32, name="wb_sb", align_bytes=64, offset=14336)
-        ws_sb = reuse.tile([P, N], U32, name="ws_sb", align_bytes=64, offset=8704)
-        sx_sb = reuse.tile([P, J], U16, name="sx_sb", align_bytes=64, offset=8192)
+        wb_sb = reuse.tile([P, N], U32, name="wb_sb", align_bytes=64, offset=14592)
+        ws_sb = reuse.tile([P, N], U32, name="ws_sb", align_bytes=64, offset=13568)
+        sx_sb = reuse.tile([P, J], U16, name="sx_sb", align_bytes=64, offset=4096)
         early = keep.tile([P, 2 * J + 2 * R], U8, name="early", align_bytes=64)
-        late = keep.tile([P, 2 * N + J], U8, name="late", align_bytes=64)
+        late_in = keep.tile([SCALE_ROWS, 2 * N + J], U8, name="late_in", align_bytes=64)
+        late = reuse.tile([P, 2 * N + J], U8, name="late", align_bytes=64, offset=12800)
         slope = keep.tile([P, PACK], F32, name="slope")
         offset = keep.tile([P, PACK], F32, name="offset")
         ident = keep.tile([P, P], F32, name="ident")
         tg_win = [keep.tile([P, T], F32, name="tg_win0")]
-        tg_win.extend(reuse.tile([P, T], F32, name="tg_win%d" % t, align_bytes=64, offset=(0, 4096, 9728)[t - 1]) for t in range(1, PACK))
+        tg_win.extend(reuse.tile([P, T], F32, name="tg_win%d" % t, align_bytes=64, offset=(0, 4608, 8704)[t - 1]) for t in range(1, PACK))
         gate = keep.tile([P, PACK, J], F32, name="gate", align_bytes=64)
 
         xt_cols, xo_cols = slice(0, J), slice(J, 2 * J)
@@ -77,8 +76,7 @@ def tile_list_crossed_tablegate_skip_plain_kernel(
 
         nc.vector.memset(xts_win[0:TOP, :].bitcast(I32), 0)
         nc.vector.memset(xos_win[0:TOP, :].bitcast(I32), 0)
-        nc.vector.memset(early[0:TOP, 2 * J :].bitcast(I32), 0)
-        nc.gpsimd.memset(late[:].bitcast(I32), 0)
+        nc.gpsimd.memset(early[0:TOP, 2 * J :].bitcast(I32), 0)
 
         nc.sync.dma_start(list_t[:], offs)
         nc.scalar.dma_start(out=xts_win[TOP:P, :].bitcast(I32), in_=xt_scales[0].bitcast(I32))
@@ -90,28 +88,31 @@ def tile_list_crossed_tablegate_skip_plain_kernel(
         nc.sync.dma_start(out=xo_win[:].bitcast(I32), in_=xo_words[0].bitcast(I32))
         nc.sync.dma_start(out=w_sb[:].bitcast(I32), in_=words8(w_words))
         nc.sync.dma_start(out=w2_sb[:].bitcast(I32), in_=words8(w2_words))
-        nc.sync.dma_start(list_g[:], offs3)
 
         nc.gpsimd.dma_start(out=slope[:], in_=sg.rearrange("(p t) o -> p (t o)", t=PACK))
         nc.gpsimd.dma_start(out=offset[:], in_=bg.rearrange("(p t) o -> p (t o)", t=PACK))
         for at, scales in ((wb_at, wb_scales), (ws_at, ws_scales), (sx_at, sx_scales)):
-            nc.gpsimd.dma_start(out=late[0:SCALE_ROWS, at : at + N].bitcast(I32), in_=scales[0].bitcast(I32))
+            nc.gpsimd.dma_start(out=late_in[:, at : at + N].bitcast(I32), in_=scales[0].bitcast(I32))
         make_identity(nc, ident[:])
-        spread_rows(nc.gpsimd, late, 0)
 
         nc.vector.tensor_copy(xts_got[:], xts_win[:].indirect(list_t[:]))
         nc.vector.tensor_copy(xos_got[:], xos_win[:].indirect(list_o[:]))
         nc.vector.tensor_copy(early[:, xt_cols].bitcast(I32), xts_got[:].bitcast(I32))
         nc.vector.tensor_copy(early[:, xo_cols].bitcast(I32), xos_got[:].bitcast(I32))
-        spread_rows(nc.scalar, early, TOP)
+        spread_rows(nc.scalar, early, early, TOP)
         nc.vector.tensor_copy(xt_got[:], xt_win[:].indirect(list_t[:]))
         nc.vector.tensor_copy(xo_got[:], xo_win[:].indirect(list_o[:]))
 
         tg_rows = tg.rearrange("(p t) q -> p t q", t=PACK)
         for t in range(PACK):
             nc.sync.dma_start(out=tg_win[t][:], in_=tg_rows[:, t, :])
+            if t == 0:
+                nc.sync.dma_start(list_g[:], offs3)
         nc.sync.dma_start(out=ws_sb[:].bitcast(I32), in_=words8(ws_words))
         nc.sync.dma_start(out=sx_sb[:].bitcast(I32), in_=sx_words[0].bitcast(I32))
+        nc.sync.dma_start(out=wb_sb[:].bitcast(I32), in_=words8(wb_words))
+        nc.gpsimd.memset(late[:].bitcast(I32), 0)
+        spread_rows(nc.sync, late, late_in, 0)
 
         for t in range(PACK):
             nc.scalar.activation(
@@ -131,12 +132,11 @@ def tile_list_crossed_tablegate_skip_plain_kernel(
             for acc, with_xt, with_xo in ((a_ps, w_op, w2_op), (b_ps, w2_op, w_op)):
                 nc.tensor.matmul_mx(out=acc[:], lhsT=xt_op[0], lhsT_scale=xt_op[1], rhs=with_xt[0], rhs_scale=with_xt[1], start=True, stop=False)
                 nc.tensor.matmul_mx(out=acc[:], lhsT=xo_op[0], lhsT_scale=xo_op[1], rhs=with_xo[0], rhs_scale=with_xo[1], start=False, stop=True)
-            a_sb = reuse.tile([P, PACK, P], F32, name="a_sb%d" % h, align_bytes=64, offset=14336 + 2048 * h)
+            a_sb = keep.tile([P, PACK, P], F32, name="a_sb%d" % h)
             larger = keep.tile([P, PACK, P], F32, name="larger%d" % h)
             nc.vector.tensor_copy(a_sb[:], a_ps[:].rearrange("j (m t) -> j t m", t=PACK))
             nc.vector.tensor_tensor(larger[:], b_ps[:].rearrange("j (m t) -> j t m", t=PACK), a_sb[:], ALU.max)
             turned.append(larger)
-        nc.sync.dma_start(out=wb_sb[:].bitcast(I32), in_=words8(wb_words))
 
         out_rows = out.rearrange("(c p) j -> p c j", p=P)
         backs = []

@@ -48,7 +48,7 @@ def tile_list_crossed_tablegate_skip_plain_kernel(
         list_o = keep.tile([P, J // 16], U16, name="list_o")
         list_g = keep.tile([P, J // 16], U16, name="list_g")
         xt_win = reuse.tile([P, T], U32, name="xt_win", align_bytes=64, offset=2048)
-        xo_win = reuse.tile([P, T], U16, name="xo_win", align_bytes=64, offset=12736)
+        xo_win = reuse.tile([P, T], U16, name="xo_win", align_bytes=64, offset=12992)
         xts_win = keep.tile([P, T], U8, name="xts_win", align_bytes=64)
         xos_win = keep.tile([P, T], U8, name="xos_win", align_bytes=64)
         xt_got = keep.tile([P, J], U32, name="xt_got", align_bytes=64)
@@ -59,15 +59,15 @@ def tile_list_crossed_tablegate_skip_plain_kernel(
         w2_sb = keep.tile([P, R], U32, name="w2_sb", align_bytes=64)
         wb_sb = reuse.tile([P, N], U32, name="wb_sb", align_bytes=64, offset=14592)
         ws_sb = reuse.tile([P, N], U32, name="ws_sb", align_bytes=64, offset=13568)
-        sx_sb = reuse.tile([P, J], U16, name="sx_sb", align_bytes=64, offset=4096)
+        sx_sb = reuse.tile([P, J], U16, name="sx_sb", align_bytes=64, offset=13056)
         early = keep.tile([P, 2 * J + 2 * R], U8, name="early", align_bytes=64)
-        late_in = keep.tile([SCALE_ROWS, 2 * N + J], U8, name="late_in", align_bytes=64)
-        late = reuse.tile([P, 2 * N + J], U8, name="late", align_bytes=64, offset=12800)
+        late_in = reuse.tile([SCALE_ROWS, 2 * N + J], U8, name="late_in", align_bytes=64, offset=4096)
+        late = keep.tile([P, 2 * N + J], U8, name="late", align_bytes=64)
         slope = keep.tile([P, PACK], F32, name="slope")
         offset = keep.tile([P, PACK], F32, name="offset")
         ident = keep.tile([P, P], F32, name="ident")
         tg_win = [keep.tile([P, T], F32, name="tg_win0")]
-        tg_win.extend(reuse.tile([P, T], F32, name="tg_win%d" % t, align_bytes=64, offset=(0, 4608, 8704)[t - 1]) for t in range(1, PACK))
+        tg_win.extend(reuse.tile([P, T], F32, name="tg_win%d" % t, align_bytes=64, offset=(0, 4864, 8960)[t - 1]) for t in range(1, PACK))
         gate = keep.tile([P, PACK, J], F32, name="gate", align_bytes=64)
 
         xt_cols, xo_cols = slice(0, J), slice(J, 2 * J)
@@ -76,7 +76,8 @@ def tile_list_crossed_tablegate_skip_plain_kernel(
 
         nc.vector.memset(xts_win[0:TOP, :].bitcast(I32), 0)
         nc.vector.memset(xos_win[0:TOP, :].bitcast(I32), 0)
-        nc.gpsimd.memset(early[0:TOP, 2 * J :].bitcast(I32), 0)
+        nc.vector.memset(early[0:TOP, 2 * J :].bitcast(I32), 0)
+        nc.vector.memset(late[:].bitcast(I32), 0)
 
         nc.sync.dma_start(list_t[:], offs)
         nc.scalar.dma_start(out=xts_win[TOP:P, :].bitcast(I32), in_=xt_scales[0].bitcast(I32))
@@ -88,30 +89,28 @@ def tile_list_crossed_tablegate_skip_plain_kernel(
         nc.sync.dma_start(out=xo_win[:].bitcast(I32), in_=xo_words[0].bitcast(I32))
         nc.sync.dma_start(out=w_sb[:].bitcast(I32), in_=words8(w_words))
         nc.sync.dma_start(out=w2_sb[:].bitcast(I32), in_=words8(w2_words))
+        nc.sync.dma_start(list_g[:], offs3)
 
         nc.gpsimd.dma_start(out=slope[:], in_=sg.rearrange("(p t) o -> p (t o)", t=PACK))
         nc.gpsimd.dma_start(out=offset[:], in_=bg.rearrange("(p t) o -> p (t o)", t=PACK))
-        for at, scales in ((wb_at, wb_scales), (ws_at, ws_scales), (sx_at, sx_scales)):
-            nc.gpsimd.dma_start(out=late_in[:, at : at + N].bitcast(I32), in_=scales[0].bitcast(I32))
         make_identity(nc, ident[:])
 
         nc.vector.tensor_copy(xts_got[:], xts_win[:].indirect(list_t[:]))
         nc.vector.tensor_copy(xos_got[:], xos_win[:].indirect(list_o[:]))
         nc.vector.tensor_copy(early[:, xt_cols].bitcast(I32), xts_got[:].bitcast(I32))
         nc.vector.tensor_copy(early[:, xo_cols].bitcast(I32), xos_got[:].bitcast(I32))
-        spread_rows(nc.scalar, early, early, TOP)
+        spread_rows(nc.sync, early, early, TOP)
         nc.vector.tensor_copy(xt_got[:], xt_win[:].indirect(list_t[:]))
         nc.vector.tensor_copy(xo_got[:], xo_win[:].indirect(list_o[:]))
 
         tg_rows = tg.rearrange("(p t) q -> p t q", t=PACK)
         for t in range(PACK):
             nc.sync.dma_start(out=tg_win[t][:], in_=tg_rows[:, t, :])
-            if t == 0:
-                nc.sync.dma_start(list_g[:], offs3)
+        for at, scales in ((wb_at, wb_scales), (ws_at, ws_scales), (sx_at, sx_scales)):
+            nc.sync.dma_start(out=late_in[:, at : at + N].bitcast(I32), in_=scales[0].bitcast(I32))
         nc.sync.dma_start(out=ws_sb[:].bitcast(I32), in_=words8(ws_words))
         nc.sync.dma_start(out=sx_sb[:].bitcast(I32), in_=sx_words[0].bitcast(I32))
         nc.sync.dma_start(out=wb_sb[:].bitcast(I32), in_=words8(wb_words))
-        nc.gpsimd.memset(late[:].bitcast(I32), 0)
         spread_rows(nc.sync, late, late_in, 0)
 
         for t in range(PACK):
@@ -135,7 +134,9 @@ def tile_list_crossed_tablegate_skip_plain_kernel(
             a_sb = keep.tile([P, PACK, P], F32, name="a_sb%d" % h)
             larger = keep.tile([P, PACK, P], F32, name="larger%d" % h)
             nc.vector.tensor_copy(a_sb[:], a_ps[:].rearrange("j (m t) -> j t m", t=PACK))
-            nc.vector.tensor_tensor(larger[:], b_ps[:].rearrange("j (m t) -> j t m", t=PACK), a_sb[:], ALU.max)
+            b_dealt = b_ps[:].rearrange("j (m t) -> j t m", t=PACK)
+            for ts in ((slice(0, 4),), (slice(0, 2), slice(2, 4)))[h]:
+                nc.vector.tensor_tensor(larger[:, ts, :], b_dealt[:, ts, :], a_sb[:, ts, :], ALU.max)
             turned.append(larger)
 
         out_rows = out.rearrange("(c p) j -> p c j", p=P)
@@ -149,7 +150,10 @@ def tile_list_crossed_tablegate_skip_plain_kernel(
             js = slice(h * HALF, (h + 1) * HALF)
             back = backs[h]
             hid = keep.tile([P, HALF, PACK], BF16, name="hid%d" % h, align_bytes=64)
-            nc.vector.tensor_tensor(hid[:], back[:].rearrange("p t j -> p j t"), gate[:, :, js].rearrange("p t j -> p j t"), ALU.mult)
+            nc.vector.tensor_tensor(
+                hid[:].rearrange("p (b i) t -> p b t i", i=4), back[:].rearrange("p t (b i) -> p b t i", i=4),
+                gate[:, :, js].rearrange("p t (b i) -> p b t i", i=4), ALU.mult,
+            )
             codes = keep.tile([P, HALF], U32, name="codes%d" % h, align_bytes=64)
             plane = keep.tile([P, HALF], U8, name="plane%d" % h, align_bytes=64)
             nc.vector.quantize_mx(out=codes[:].bitcast(E4M3), scales=plane[:], in_=hid[:].rearrange("p j t -> p (j t)"))

@@ -73,6 +73,7 @@ def tile_list_crossed_tablegate_skip_plain_kernel(
         xt_cols, xo_cols = slice(0, J), slice(J, 2 * J)
         w_cols, w2_cols = slice(2 * J, 2 * J + R), slice(2 * J + R, 2 * J + 2 * R)
         wb_at, ws_at, sx_at = 0, N, 2 * N
+        tg_rows = tg.rearrange("(p t) q -> p t q", t=PACK)
 
         nc.vector.memset(xts_win[0:TOP, :].bitcast(I32), 0)
         nc.vector.memset(xos_win[0:TOP, :].bitcast(I32), 0)
@@ -86,10 +87,11 @@ def tile_list_crossed_tablegate_skip_plain_kernel(
         nc.sync.dma_start(out=xt_win[:].bitcast(I32), in_=words8(xt_words))
         nc.scalar.dma_start(out=early[TOP:P, w_cols].bitcast(I32), in_=w_scales[0].bitcast(I32))
         nc.scalar.dma_start(out=early[TOP:P, w2_cols].bitcast(I32), in_=w2_scales[0].bitcast(I32))
+        nc.sync.dma_start(out=tg_win[0][:], in_=tg_rows[:, 0, :])
+        nc.sync.dma_start(list_g[:], offs3)
         nc.sync.dma_start(out=xo_win[:].bitcast(I32), in_=xo_words[0].bitcast(I32))
         nc.sync.dma_start(out=w_sb[:].bitcast(I32), in_=words8(w_words))
         nc.sync.dma_start(out=w2_sb[:].bitcast(I32), in_=words8(w2_words))
-        nc.sync.dma_start(list_g[:], offs3)
 
         nc.gpsimd.dma_start(out=slope[:], in_=sg.rearrange("(p t) o -> p (t o)", t=PACK))
         nc.gpsimd.dma_start(out=offset[:], in_=bg.rearrange("(p t) o -> p (t o)", t=PACK))
@@ -103,11 +105,11 @@ def tile_list_crossed_tablegate_skip_plain_kernel(
         nc.vector.tensor_copy(xt_got[:], xt_win[:].indirect(list_t[:]))
         nc.vector.tensor_copy(xo_got[:], xo_win[:].indirect(list_o[:]))
 
-        tg_rows = tg.rearrange("(p t) q -> p t q", t=PACK)
-        for t in range(PACK):
+        for t in range(1, PACK):
             nc.sync.dma_start(out=tg_win[t][:], in_=tg_rows[:, t, :])
-        for at, scales in ((wb_at, wb_scales), (ws_at, ws_scales), (sx_at, sx_scales)):
-            nc.sync.dma_start(out=late_in[:, at : at + N].bitcast(I32), in_=scales[0].bitcast(I32))
+            if t == 2:
+                for at, scales in ((wb_at, wb_scales), (ws_at, ws_scales), (sx_at, sx_scales)):
+                    nc.sync.dma_start(out=late_in[:, at : at + N].bitcast(I32), in_=scales[0].bitcast(I32))
         nc.sync.dma_start(out=ws_sb[:].bitcast(I32), in_=words8(ws_words))
         nc.sync.dma_start(out=sx_sb[:].bitcast(I32), in_=sx_words[0].bitcast(I32))
         nc.sync.dma_start(out=wb_sb[:].bitcast(I32), in_=words8(wb_words))
@@ -127,16 +129,22 @@ def tile_list_crossed_tablegate_skip_plain_kernel(
             w_op = (w_sb[:].bitcast(E5M2), early[:, w_cols])
             w2_op = (w2_sb[:].bitcast(E5M2), early[:, w2_cols])
             a_ps = psum.tile([P, R], F32, name="a_ps%d" % h)
-            b_ps = psum.tile([P, R], F32, name="b_ps%d" % h, tag="b_ps%d" % h)
-            for acc, with_xt, with_xo in ((a_ps, w_op, w2_op), (b_ps, w2_op, w_op)):
-                nc.tensor.matmul_mx(out=acc[:], lhsT=xt_op[0], lhsT_scale=xt_op[1], rhs=with_xt[0], rhs_scale=with_xt[1], start=True, stop=False)
-                nc.tensor.matmul_mx(out=acc[:], lhsT=xo_op[0], lhsT_scale=xo_op[1], rhs=with_xo[0], rhs_scale=with_xo[1], start=False, stop=True)
+            nc.tensor.matmul_mx(out=a_ps[:], lhsT=xt_op[0], lhsT_scale=xt_op[1], rhs=w_op[0], rhs_scale=w_op[1], start=True, stop=False)
+            nc.tensor.matmul_mx(out=a_ps[:], lhsT=xo_op[0], lhsT_scale=xo_op[1], rhs=w2_op[0], rhs_scale=w2_op[1], start=False, stop=True)
             a_sb = keep.tile([P, PACK, P], F32, name="a_sb%d" % h)
             larger = keep.tile([P, PACK, P], F32, name="larger%d" % h)
             nc.vector.tensor_copy(a_sb[:], a_ps[:].rearrange("j (m t) -> j t m", t=PACK))
-            b_dealt = b_ps[:].rearrange("j (m t) -> j t m", t=PACK)
-            for ts in ((slice(0, 4),), (slice(0, 2), slice(2, 4)))[h]:
-                nc.vector.tensor_tensor(larger[:, ts, :], b_dealt[:, ts, :], a_sb[:, ts, :], ALU.max)
+            parts = h + 1
+            width = R // parts
+            for part in range(parts):
+                rs = slice(part * width, (part + 1) * width)
+                ms = slice(part * width // PACK, (part + 1) * width // PACK)
+                b_ps = psum.tile([P, width], F32, name="b_ps%d_%d" % (h, part), tag="b_ps%d_%d" % (h, part))
+                nc.tensor.matmul_mx(out=b_ps[:], lhsT=xt_op[0], lhsT_scale=xt_op[1], rhs=w2_sb[:, rs].bitcast(E5M2), rhs_scale=w2_op[1][:, rs], start=True, stop=False)
+                nc.tensor.matmul_mx(out=b_ps[:], lhsT=xo_op[0], lhsT_scale=xo_op[1], rhs=w_sb[:, rs].bitcast(E5M2), rhs_scale=w_op[1][:, rs], start=False, stop=True)
+                b_dealt = b_ps[:].rearrange("j (m t) -> j t m", t=PACK)
+                for ts in ((slice(0, 4),), (slice(0, 2), slice(2, 4)))[part]:
+                    nc.vector.tensor_tensor(larger[:, ts, ms], b_dealt[:, ts, :], a_sb[:, ts, ms], ALU.max)
             turned.append(larger)
 
         out_rows = out.rearrange("(c p) j -> p c j", p=P)
@@ -157,21 +165,36 @@ def tile_list_crossed_tablegate_skip_plain_kernel(
             codes = keep.tile([P, HALF], U32, name="codes%d" % h, align_bytes=64)
             plane = keep.tile([P, HALF], U8, name="plane%d" % h, align_bytes=64)
             nc.vector.quantize_mx(out=codes[:].bitcast(E4M3), scales=plane[:], in_=hid[:].rearrange("p j t -> p (j t)"))
-            y_ps = psum.tile([P, N // P, HALF], F32, name="y_ps%d" % h, tag=("b_ps1", "back0")[h])
-            for c in range(N // P):
+            def own(c, acc, start):
                 nc.tensor.matmul_mx(
-                    out=y_ps[:, c, :], lhsT=ws_sb[:, c * P : (c + 1) * P].bitcast(E5M2), lhsT_scale=late[:, ws_at + c * P : ws_at + (c + 1) * P],
-                    rhs=sx_sb[:, js].bitcast(E2M1), rhs_scale=late[:, sx_at + h * HALF : sx_at + (h + 1) * HALF], start=(c == 0), stop=False,
+                    out=acc, lhsT=ws_sb[:, c * P : (c + 1) * P].bitcast(E5M2), lhsT_scale=late[:, ws_at + c * P : ws_at + (c + 1) * P],
+                    rhs=sx_sb[:, js].bitcast(E2M1), rhs_scale=late[:, sx_at + h * HALF : sx_at + (h + 1) * HALF], start=start, stop=False,
                 )
-            for c in range(N // P):
+
+            def hidden(c, acc, stop):
                 nc.tensor.matmul_mx(
-                    out=y_ps[:, c, :], lhsT=wb_sb[:, c * P : (c + 1) * P].bitcast(E5M2), lhsT_scale=late[:, wb_at + c * P : wb_at + (c + 1) * P],
-                    rhs=codes[:].bitcast(E4M3), rhs_scale=plane[:], start=False, stop=(c == N // P - 1),
+                    out=acc, lhsT=wb_sb[:, c * P : (c + 1) * P].bitcast(E5M2), lhsT_scale=late[:, wb_at + c * P : wb_at + (c + 1) * P],
+                    rhs=codes[:].bitcast(E4M3), rhs_scale=plane[:], start=False, stop=stop,
                 )
-            y_sb = keep.tile([P, N // P, HALF], F32, name="y_sb%d" % h)
+
             if h == 0:
+                y_ps = psum.tile([P, N // P, HALF], F32, name="y_ps0", tag="b_ps1_1")
+                for c in range(N // P):
+                    own(c, y_ps[:, c, :], c == 0)
+                for c in range(N // P):
+                    hidden(c, y_ps[:, c, :], c == N // P - 1)
+                y_sb = keep.tile([P, N // P, HALF], F32, name="y_sb0")
                 nc.scalar.copy(y_sb[:], y_ps[:])
                 nc.scalar.dma_start(out=out_rows[:, :, js], in_=y_sb[:])
             else:
-                nc.vector.tensor_copy(y_sb[:], y_ps[:])
-                nc.sync.dma_start(out=out_rows[:, :, js], in_=y_sb[:])
+                accs = [psum.tile([P, HALF], F32, name="y_ps1_%d" % c, tag="back%d" % c) for c in range(N // P)]
+                for c in range(N // P):
+                    own(c, accs[c][:], True)
+                for c in range(N // P):
+                    hidden(c, accs[c][:], True)
+                y_lo = keep.tile([P, HALF], F32, name="y_lo")
+                y_hi = keep.tile([P, HALF], F32, name="y_hi")
+                nc.scalar.copy(y_lo[:], accs[0][:])
+                nc.scalar.dma_start(out=out_rows[:, 0, js], in_=y_lo[:])
+                nc.vector.tensor_copy(y_hi[:], accs[1][:])
+                nc.sync.dma_start(out=out_rows[:, 1, js], in_=y_hi[:])

@@ -113,7 +113,7 @@ def tile_list_crossed_tablegate_skip_plain_kernel(
         nc.sync.dma_start(out=ws_sb[:].bitcast(I32), in_=words8(ws_words))
         nc.sync.dma_start(out=sx_sb[:].bitcast(I32), in_=sx_words[0].bitcast(I32))
         nc.sync.dma_start(out=wb_sb[:].bitcast(I32), in_=words8(wb_words))
-        spread_rows(nc.sync, late, late_in, 0)
+        spread_rows(nc.scalar, late, late_in, 0)
 
         for t in range(PACK):
             nc.scalar.activation(

from contextlib import ExitStack

import concourse.mybir as mybir
from concourse.masks import make_identity

K, T, J, R, N = 512, 1024, 256, 512, 256
FLOPS = 2 * K * (4 * R * J + 2 * N * J)

F32 = mybir.dt.float32
BF16 = mybir.dt.bfloat16
I32 = mybir.dt.int32
U32 = mybir.dt.uint32
U16 = mybir.dt.uint16
U8 = mybir.dt.uint8
E4M3 = mybir.dt.float8_e4m3fn_x4
E5M2 = mybir.dt.float8_e5m2_x4
E2M1 = mybir.dt.float4_e2m1fn_x4
ALU = mybir.AluOpType
ACT = mybir.ActivationFunctionType

P = 128
PACK = 4
HALF = 128
SCALE_ROWS = 16
TOP = P - SCALE_ROWS


def tile_list_crossed_tablegate_skip_plain_kernel(
    tc, xt_words, xt_scales, xo_words, xo_scales, w_words, w_scales, w2_words, w2_scales, tg, sg, bg,
    wb_words, wb_scales, sx_words, sx_scales, ws_words, ws_scales, offs, offs2, offs3, out,
):
    nc = tc.nc

    def words8(dram):
        return dram[0].rearrange("p n t -> p (n t)").bitcast(I32)

    def spread_rows(queue, planes, source, first_row):
        for q in range(4):
            row = first_row + 4 * q
            queue.dma_start(out=planes[32 * q : 32 * q + 4, :].bitcast(I32), in_=source[row : row + 4, :].bitcast(I32))

    with ExitStack() as ctx:
        keep = ctx.enter_context(tc.tile_pool(name="keep", bufs=1))
        reuse = ctx.enter_context(tc.tile_pool(name="reuse", bufs=1))
        psum = ctx.enter_context(tc.psum_pool(name="psum", bufs=1))

        list_t = keep.tile([P, J // 16], U16, name="list_t")
        list_o = keep.tile([P, J // 16], U16, name="list_o")
        list_g = keep.tile([P, J // 16], U16, name="list_g")
        xt_win = reuse.tile([P, T], U32, name="xt_win", align_bytes=64, offset=2048)
        xo_win = reuse.tile([P, T], U16, name="xo_win", align_bytes=64, offset=12992)
        xts_win = keep.tile([P, T], U8, name="xts_win", align_bytes=64)
        xos_win = keep.tile([P, T], U8, name="xos_win", align_bytes=64)
        xt_got = keep.tile([P, J], U32, name="xt_got", align_bytes=64)
        xo_got = keep.tile([P, J], U16, name="xo_got", align_bytes=64)
        xts_got = keep.tile([P, J], U8, name="xts_got", align_bytes=64)
        xos_got = keep.tile([P, J], U8, name="xos_got", align_bytes=64)
        w_sb = keep.tile([P, R], U32, name="w_sb", align_bytes=64)
        w2_sb = keep.tile([P, R], U32, name="w2_sb", align_bytes=64)
        wb_sb = reuse.tile([P, N], U32, name="wb_sb", align_bytes=64, offset=14592)
        ws_sb = reuse.tile([P, N], U32, name="ws_sb", align_bytes=64, offset=13568)
        sx_sb = reuse.tile([P, J], U16, name="sx_sb", align_bytes=64, offset=13056)
        early = keep.tile([P, 2 * J + 2 * R], U8, name="early", align_bytes=64)
        late_in = reuse.tile([SCALE_ROWS, 2 * N + J], U8, name="late_in", align_bytes=64, offset=4096)
        late = keep.tile([P, 2 * N + J], U8, name="late", align_bytes=64)
        slope = keep.tile([P, PACK], F32, name="slope")
        offset = keep.tile([P, PACK], F32, name="offset")
        ident = keep.tile([P, P], F32, name="ident")
        tg_win = [keep.tile([P, T], F32, name="tg_win0")]
        tg_win.extend(reuse.tile([P, T], F32, name="tg_win%d" % t, align_bytes=64, offset=(0, 4864, 8960)[t - 1]) for t in range(1, PACK))
        gate = keep.tile([P, PACK, J], F32, name="gate", align_bytes=64)

        xt_cols, xo_cols = slice(0, J), slice(J, 2 * J)
        w_cols, w2_cols = slice(2 * J, 2 * J + R), slice(2 * J + R, 2 * J + 2 * R)
        wb_at, ws_at, sx_at = 0, N, 2 * N
        tg_rows = tg.rearrange("(p t) q -> p t q", t=PACK)

        nc.vector.memset(xts_win[0:TOP, :].bitcast(I32), 0)
        nc.vector.memset(xos_win[0:TOP, :].bitcast(I32), 0)
        nc.vector.memset(early[0:TOP, 2 * J :].bitcast(I32), 0)
        nc.vector.memset(late[:].bitcast(I32), 0)

        nc.sync.dma_start(list_t[:], offs)
        nc.scalar.dma_start(out=xts_win[TOP:P, :].bitcast(I32), in_=xt_scales[0].bitcast(I32))
        nc.sync.dma_start(list_o[:], offs2)
        nc.scalar.dma_start(out=xos_win[TOP:P, :].bitcast(I32), in_=xo_scales[0].bitcast(I32))
        nc.sync.dma_start(out=xt_win[:].bitcast(I32), in_=words8(xt_words))
        nc.scalar.dma_start(out=early[TOP:P, w_cols].bitcast(I32), in_=w_scales[0].bitcast(I32))
        nc.scalar.dma_start(out=early[TOP:P, w2_cols].bitcast(I32), in_=w2_scales[0].bitcast(I32))
        nc.sync.dma_start(out=tg_win[0][:], in_=tg_rows[:, 0, :])
        nc.sync.dma_start(list_g[:], offs3)
        nc.sync.dma_start(out=xo_win[:].bitcast(I32), in_=xo_words[0].bitcast(I32))
        nc.sync.dma_start(out=w_sb[:].bitcast(I32), in_=words8(w_words))
        nc.sync.dma_start(out=w2_sb[:].bitcast(I32), in_=words8(w2_words))

        nc.gpsimd.dma_start(out=slope[:], in_=sg.rearrange("(p t) o -> p (t o)", t=PACK))
        nc.gpsimd.dma_start(out=offset[:], in_=bg.rearrange("(p t) o -> p (t o)", t=PACK))
        make_identity(nc, ident[:])

        nc.vector.tensor_copy(xts_got[:], xts_win[:].indirect(list_t[:]))
        nc.vector.tensor_copy(xos_got[:], xos_win[:].indirect(list_o[:]))
        nc.vector.tensor_copy(early[:, xt_cols].bitcast(I32), xts_got[:].bitcast(I32))
        nc.vector.tensor_copy(early[:, xo_cols].bitcast(I32), xos_got[:].bitcast(I32))
        spread_rows(nc.sync, early, early, TOP)
        nc.vector.tensor_copy(xt_got[:], xt_win[:].indirect(list_t[:]))
        nc.vector.tensor_copy(xo_got[:], xo_win[:].indirect(list_o[:]))

        for t in range(1, PACK):
            nc.sync.dma_start(out=tg_win[t][:], in_=tg_rows[:, t, :])
            if t == 2:
                for at, scales in ((wb_at, wb_scales), (ws_at, ws_scales), (sx_at, sx_scales)):
                    nc.sync.dma_start(out=late_in[:, at : at + N].bitcast(I32), in_=scales[0].bitcast(I32))
        nc.sync.dma_start(out=ws_sb[:].bitcast(I32), in_=words8(ws_words))
        nc.sync.dma_start(out=sx_sb[:].bitcast(I32), in_=sx_words[0].bitcast(I32))
        nc.sync.dma_start(out=wb_sb[:].bitcast(I32), in_=words8(wb_words))
        spread_rows(nc.scalar, late, late_in, 0)

        for t in range(PACK):
            nc.scalar.activation(
                out=gate[:, t, :], in_=tg_win[t][:].indirect(list_g[:]), func=ACT.Sigmoid,
                bias=offset[:, t : t + 1], scale=slope[:, t : t + 1],
            )

        turned = []
        for h in range(J // HALF):
            js = slice(h * HALF, (h + 1) * HALF)
            xt_op = (xt_got[:, js].bitcast(E4M3), early[:, h * HALF : (h + 1) * HALF])
            xo_op = (xo_got[:, js].bitcast(E2M1), early[:, J + h * HALF : J + (h + 1) * HALF])
            w_op = (w_sb[:].bitcast(E5M2), early[:, w_cols])
            w2_op = (w2_sb[:].bitcast(E5M2), early[:, w2_cols])
            a_ps = psum.tile([P, R], F32, name="a_ps%d" % h)
            nc.tensor.matmul_mx(out=a_ps[:], lhsT=xt_op[0], lhsT_scale=xt_op[1], rhs=w_op[0], rhs_scale=w_op[1], start=True, stop=False)
            nc.tensor.matmul_mx(out=a_ps[:], lhsT=xo_op[0], lhsT_scale=xo_op[1], rhs=w2_op[0], rhs_scale=w2_op[1], start=False, stop=True)
            a_sb = keep.tile([P, PACK, P], F32, name="a_sb%d" % h)
            larger = keep.tile([P, PACK, P], F32, name="larger%d" % h)
            nc.vector.tensor_copy(a_sb[:], a_ps[:].rearrange("j (m t) -> j t m", t=PACK))
            parts = h + 1
            width = R // parts
            for part in range(parts):
                rs = slice(part * width, (part + 1) * width)
                ms = slice(part * width // PACK, (part + 1) * width // PACK)
                b_ps = psum.tile([P, width], F32, name="b_ps%d_%d" % (h, part), tag="b_ps%d_%d" % (h, part))
                nc.tensor.matmul_mx(out=b_ps[:], lhsT=xt_op[0], lhsT_scale=xt_op[1], rhs=w2_sb[:, rs].bitcast(E5M2), rhs_scale=w2_op[1][:, rs], start=True, stop=False)
                nc.tensor.matmul_mx(out=b_ps[:], lhsT=xo_op[0], lhsT_scale=xo_op[1], rhs=w_sb[:, rs].bitcast(E5M2), rhs_scale=w_op[1][:, rs], start=False, stop=True)
                b_dealt = b_ps[:].rearrange("j (m t) -> j t m", t=PACK)
                for ts in ((slice(0, 4),), (slice(0, 2), slice(2, 4)))[part]:
                    nc.vector.tensor_tensor(larger[:, ts, ms], b_dealt[:, ts, :], a_sb[:, ts, ms], ALU.max)
            turned.append(larger)

        out_rows = out.rearrange("(c p) j -> p c j", p=P)
        backs = []
        for h in range(J // HALF):
            back = psum.tile([P, PACK, HALF], F32, name="back%d" % h, tag="back%d" % h)
            for t in range(PACK):
                nc.tensor.transpose(back[:, t, :], turned[h][:, t, :], ident[:])
            backs.append(back)
        for h in range(J // HALF):
            js = slice(h * HALF, (h + 1) * HALF)
            back = backs[h]
            hid = keep.tile([P, HALF, PACK], BF16, name="hid%d" % h, align_bytes=64)
            nc.vector.tensor_tensor(
                hid[:].rearrange("p (b i) t -> p b t i", i=4), back[:].rearrange("p t (b i) -> p b t i", i=4),
                gate[:, :, js].rearrange("p t (b i) -> p b t i", i=4), ALU.mult,
            )
            codes = keep.tile([P, HALF], U32, name="codes%d" % h, align_bytes=64)
            plane = keep.tile([P, HALF], U8, name="plane%d" % h, align_bytes=64)
            nc.vector.quantize_mx(out=codes[:].bitcast(E4M3), scales=plane[:], in_=hid[:].rearrange("p j t -> p (j t)"))
            def own(c, acc, start):
                nc.tensor.matmul_mx(
                    out=acc, lhsT=ws_sb[:, c * P : (c + 1) * P].bitcast(E5M2), lhsT_scale=late[:, ws_at + c * P : ws_at + (c + 1) * P],
                    rhs=sx_sb[:, js].bitcast(E2M1), rhs_scale=late[:, sx_at + h * HALF : sx_at + (h + 1) * HALF], start=start, stop=False,
                )

            def hidden(c, acc, stop):
                nc.tensor.matmul_mx(
                    out=acc, lhsT=wb_sb[:, c * P : (c + 1) * P].bitcast(E5M2), lhsT_scale=late[:, wb_at + c * P : wb_at + (c + 1) * P],
                    rhs=codes[:].bitcast(E4M3), rhs_scale=plane[:], start=False, stop=stop,
                )

            if h == 0:
                y_ps = psum.tile([P, N // P, HALF], F32, name="y_ps0", tag="b_ps1_1")
                for c in range(N // P):
                    own(c, y_ps[:, c, :], c == 0)
                for c in range(N // P):
                    hidden(c, y_ps[:, c, :], c == N // P - 1)
                y_sb = keep.tile([P, N // P, HALF], F32, name="y_sb0")
                nc.scalar.copy(y_sb[:], y_ps[:])
                nc.scalar.dma_start(out=out_rows[:, :, js], in_=y_sb[:])
            else:
                accs = [psum.tile([P, HALF], F32, name="y_ps1_%d" % c, tag="back%d" % c) for c in range(N // P)]
                for c in range(N // P):
                    own(c, accs[c][:], True)
                for c in range(N // P):
                    hidden(c, accs[c][:], True)
                y_lo = keep.tile([P, HALF], F32, name="y_lo")
                y_hi = keep.tile([P, HALF], F32, name="y_hi")
                nc.scalar.copy(y_lo[:], accs[0][:])
                nc.scalar.dma_start(out=out_rows[:, 0, js], in_=y_lo[:])
                nc.vector.tensor_copy(y_hi[:], accs[1][:])
                nc.sync.dma_start(out=out_rows[:, 1, js], in_=y_hi[:])
